import numpy as np
import ml_dtypes


def mxq(x, axis, fmt="e4m3"):
    dtype, down = {"e4m3": (ml_dtypes.float8_e4m3fn, 7), "e5m2": (ml_dtypes.float8_e5m2, 14)}[fmt]
    v = np.moveaxis(np.asarray(x, np.float32).astype(ml_dtypes.bfloat16).astype(np.float64), axis, -1)
    blocks = v.reshape(v.shape[:-1] + (-1, 32))
    amax = np.abs(blocks).max(-1, keepdims=True)
    byte = np.maximum(np.where(amax > 0, np.frexp(amax)[1] - 1 + 127, 0) - down, 1)
    scale = np.exp2(byte - 127.0)
    codes = (blocks / scale).astype(np.float32).astype(dtype).astype(np.float64)
    return np.moveaxis((codes * scale).reshape(v.shape), -1, axis)


WIDE = False


def mx_kscale(k):
    if not WIDE:
        return np.ones(k)
    levels = np.array([10, -10, 5, -5, 0])
    if k % 512:
        return np.exp2(np.random.permutation(np.resize(levels, k // 32))).repeat(32)
    a = np.empty((k // 512, 16))
    for p in range(k // 512):
        a[p, :8] = np.random.permutation(np.resize(levels, 8))
        for g in range(8):
            far = levels[np.abs(levels - a[p, g]) >= 10]
            a[p, g + 8] = far[np.random.randint(len(far))]
    return np.exp2(a.ravel()).repeat(32)


def f64(x):
    return np.asarray(x).astype(np.float64)


def striped(idx):
    return np.tile(idx.reshape(-1, 16).T, (8, 1)).astype(np.uint16)


def unstriped(offs):
    return offs[:16].T.reshape(-1).astype(np.int64)


def pack_weight(w):
    k, n = w.shape
    w = f64(np.asarray(w, np.float32).astype(ml_dtypes.bfloat16)).reshape(k // 32, 32, n)
    amax = np.abs(w).max(1)
    byte = np.clip(np.where(amax > 0, np.frexp(amax)[1] - 1 + 127 - 7, 1), 1, 254)
    scaled = (w * np.exp2(127.0 - byte)[:, None, :]).reshape(k, n).astype(np.float32)
    words = np.ascontiguousarray(scaled.reshape(k // 512, 128, 4, n).transpose(0, 1, 3, 2)).astype(ml_dtypes.float8_e4m3fn).view(np.uint8)
    return words, np.ascontiguousarray(byte.astype(np.uint8).reshape(k // 512, 16, n))


def unpack_weight(words, scales):
    g, p, n, _ = words.shape
    vals = np.ascontiguousarray(words).view(ml_dtypes.float8_e4m3fn).astype(np.float64) * np.repeat(np.exp2(scales.astype(np.float64) - 127.0), 8, axis=1)[..., None]
    return vals.transpose(0, 1, 3, 2).reshape(g * 512, n)


def relu(v):
    return np.maximum(v, 0.0)


K, T, S, V, D = 1024, 1024, 512, 256, 4
P = 2 ** 7


def setup_inputs():
    n = np.random.standard_normal
    s = mx_kscale(K)[:, None]
    packed_xT = pack_weight(n((K, T)) * s)
    return {
        "x_words": packed_xT[0],
        "x_scales": packed_xT[1],
        "hT": (n((K, V)) / np.sqrt(K) / s).astype(np.float32),
        "ment": (np.tile(0.5 * n(T), (P, 1))).astype(np.float32),
        "gold": (np.tile((np.random.uniform(size=S) < 0.4) * 0.98 + 0.01, (P, 1))).astype(np.float32),
        "offs": striped(np.random.permutation(T)[:S]),
    }


def reference(x_words, x_scales, hT, ment, gold, offs):
    hTq = mxq(f64(hT), 0, "e4m3")
    xq = unpack_weight(x_words, x_scales)[:, unstriped(offs)]
    y = (hTq.T @ xq) + f64(ment)[:1][:, unstriped(offs)]
    top = relu(y.reshape(len(y), -1, D).max(axis=2))
    ex = np.exp(y - np.repeat(top, D, axis=1))
    tot = ex.reshape(len(ex), -1, D).sum(axis=2) + np.exp(-1.0 * top)
    eg = ex * f64(gold)[:1]
    return np.log(tot) - (np.log(eg.reshape(len(eg), -1, D).sum(axis=2) + 0.001))

@@ -1,0 +1,198 @@
+from contextlib import ExitStack
+
+import concourse.mybir as mybir
+from concourse.masks import make_identity
+
+K, T, S, V, D = 1024, 1024, 512, 256, 4
+FLOPS = 2 * K * S * V
+
+F32 = mybir.dt.float32
+BF16 = mybir.dt.bfloat16
+I32 = mybir.dt.int32
+U32 = mybir.dt.uint32
+U16 = mybir.dt.uint16
+U8 = mybir.dt.uint8
+FP8X4 = mybir.dt.float8_e4m3fn_x4
+ALU = mybir.AluOpType
+ACT = mybir.ActivationFunctionType
+
+P = 128
+PACK = 4
+PASSES = K // (P * PACK)
+G = S // D
+HALVES = V // P
+PAIRS = D // 2
+EPS = 0.001
+
+
+def tile_picked_ycoref_loss_p_kernel(tc, x_words, x_scales, hT, ment, gold, offs, out):
+    nc = tc.nc
+    with ExitStack() as ctx:
+        sb = ctx.enter_context(tc.tile_pool(name="sb", bufs=1))
+        ps = ctx.enter_context(tc.psum_pool(name="ps", bufs=1))
+
+        offsets = sb.tile([P, S // 16], U16, name="offsets")
+        ment_win = sb.tile([P, T], F32, name="ment_win")
+        word_win = [sb.tile([P, T], U32, name="word_win%d" % o) for o in range(PASSES)]
+        scale_win = sb.tile([P, T], U8, name="scale_win")
+        h_raw = [sb.tile([P, PACK, V], F32, name="h_raw%d" % o) for o in range(PASSES)]
+        gold_col = sb.tile([P, D], F32, name="gold_col")
+        ident = sb.tile([P, P], F32, name="ident")
+
+        zero_col = sb.tile([P, 1], F32, name="zero_col")
+        nc.gpsimd.memset(scale_win[:].bitcast(I32), 0)
+        nc.gpsimd.memset(zero_col[:], 0.0)
+        make_identity(nc, ident[:])
+        nc.scalar.activation(out=ment_win[0 : P - 1, :], in_=zero_col[0 : P - 1, :].to_broadcast([P - 1, T]), func=ACT.Copy)
+
+        def load_words(o):
+            nc.sync.dma_start(
+                out=word_win[o][:].bitcast(I32),
+                in_=x_words[o].rearrange("p n t -> p (n t)").bitcast(I32),
+            )
+
+        def load_h(o):
+            rows = hT[o * P * PACK : (o + 1) * P * PACK, :]
+            nc.sync.dma_start(out=h_raw[o][:], in_=rows.rearrange("(p j) w -> p j w", j=PACK))
+
+        nc.sync.dma_start(offsets[:], offs)
+        nc.sync.dma_start(out=ment_win[P - 1 : P, :], in_=ment[0:1, :])
+        load_words(0)
+        for q in range(4):
+            nc.sync.dma_start(
+                out=scale_win[32 * q : 32 * q + 4 * PASSES, :].bitcast(I32),
+                in_=x_scales[:, 4 * q : 4 * q + 4, :].bitcast(I32),
+            )
+        load_h(0)
+        load_words(1)
+        load_h(1)
+        nc.sync.dma_start(out=gold_col[:], in_=gold[0:1, :].rearrange("o (g d) -> (o g) d", d=D))
+
+        ment_row = sb.tile([P, S], F32, name="ment_row")
+        nc.scalar.activation(out=ment_row[:], in_=ment_win[:].indirect(offsets[:]), func=ACT.Copy)
+        ment_ps = ps.tile([P, D, P], F32, name="ment_ps")
+        for d in range(D):
+            nc.tensor.transpose(ment_ps[:, d, :], ment_row[:].rearrange("p (g d) -> p d g", d=D)[:, d, :], ident[:])
+        ment_col = sb.tile([P, D], F32, name="ment_col")
+        nc.scalar.copy(out=ment_col[:], in_=ment_ps[:, :, P - 1])
+
+        x_code = [sb.tile([P, D, G], U32, name="x_code%d" % o, align_bytes=64) for o in range(PASSES)]
+        x_scale = sb.tile([P, D, G], U8, name="x_scale", align_bytes=64)
+        h_bf = [[sb.tile([P, P, PACK], BF16, name="h_bf%d%d" % (o, h), align_bytes=64) for h in range(HALVES)] for o in range(PASSES)]
+        h_code = [[sb.tile([P, P], U32, name="h_code%d%d" % (o, h), align_bytes=64) for h in range(HALVES)] for o in range(PASSES)]
+        h_scale = [[sb.tile([P, P], U8, name="h_scale%d%d" % (o, h), align_bytes=64) for h in range(HALVES)] for o in range(PASSES)]
+        score = [[ps.tile([P, 2, P], F32, name="score%d%d" % (h, r)) for r in range(PAIRS)] for h in range(HALVES)]
+
+        def gather_words(o):
+            nc.vector.tensor_copy(out=x_code[o][:].rearrange("p d g -> p g d"), in_=word_win[o][:].indirect(offsets[:]))
+
+        def cast(copy, o, h):
+            copy(out=h_bf[o][h][:], in_=h_raw[o][:, :, h * P : (h + 1) * P].rearrange("p j w -> p w j"))
+
+        def quant(o, h):
+            nc.vector.quantize_mx(
+                out=h_code[o][h][:].bitcast(FP8X4), scales=h_scale[o][h][:], in_=h_bf[o][h][:].rearrange("p w j -> p (w j)")
+            )
+
+        def product(o, h):
+            for d in range(D):
+                nc.tensor.matmul_mx(
+                    out=score[h][d // 2][:, d % 2, :],
+                    lhsT=x_code[o][:, d, :].bitcast(FP8X4),
+                    lhsT_scale=x_scale[4 * o : P, d, :],
+                    rhs=h_code[o][h][:].bitcast(FP8X4),
+                    rhs_scale=h_scale[o][h][:],
+                    start=(o == 0 and d % 2 == 0),
+                    stop=(o == PASSES - 1 and d % 2 == 1),
+                )
+
+        gather_words(0)
+        nc.vector.tensor_copy(out=x_scale[:].rearrange("p d g -> p g d"), in_=scale_win[:].indirect(offsets[:]))
+        cast(nc.scalar.copy, 0, 0)
+        cast(nc.scalar.copy, 0, 1)
+        gather_words(1)
+        quant(0, 0)
+        product(0, 0)
+        cast(nc.vector.tensor_copy, 1, 0)
+        cast(nc.scalar.copy, 1, 1)
+        quant(0, 1)
+        product(0, 1)
+        quant(1, 0)
+        product(1, 0)
+        quant(1, 1)
+        product(1, 1)
+
+        ex = [sb.tile([P, D + 1, P], F32, name="ex%d" % h) for h in range(HALVES)]
+        eg = [sb.tile([P, D, P], F32, name="eg%d" % h) for h in range(HALVES)]
+        tot0 = ps.tile([P, G], F32, name="tot0")
+        den0 = ps.tile([P, G], F32, name="den0")
+        sums1 = ps.tile([P, 2, G], F32, name="sums1")
+        tot = [tot0[:], sums1[:, 0, :]]
+        den = [den0[:], sums1[:, 1, :]]
+
+        diff = [sb.tile([P, D, P], F32, name="diff%d" % h) for h in range(HALVES)]
+        low = [sb.tile([P, 2, P], F32, name="low%d" % h) for h in range(HALVES)]
+        pair = [sb.tile([P, 2, P], F32, name="pair%d" % h) for h in range(HALVES)]
+        top = [sb.tile([P, P], F32, name="top%d" % h) for h in range(HALVES)]
+
+        def relu_low(h):
+            for d in range(2):
+                nc.scalar.activation(out=low[h][:, d, :], in_=score[h][0][:, d, :], func=ACT.Relu, bias=ment_col[:, d : d + 1])
+
+        def pair_max(h, i):
+            nc.vector.scalar_tensor_tensor(
+                pair[h][:, i, :], score[h][1][:, i, :], ment_col[:, 2 + i : 3 + i], low[h][:, i, :], ALU.add, ALU.max
+            )
+
+        def top_max(h):
+            nc.vector.tensor_tensor(top[h][:], pair[h][:, 0, :], pair[h][:, 1, :], ALU.max)
+            nc.scalar.activation(out=ex[h][:, D, :], in_=top[h][:], func=ACT.Exp, scale=-1.0)
+
+        def exps(h, d0, n):
+            nc.vector.tensor_tensor(
+                diff[h][:, d0 : d0 + n, :],
+                score[h][d0 // 2][:, d0 % 2 : d0 % 2 + n, :],
+                top[h][:].unsqueeze(1).to_broadcast([P, n, P]),
+                ALU.subtract,
+            )
+            for d in range(d0, d0 + n):
+                nc.scalar.activation(out=ex[h][:, d, :], in_=diff[h][:, d, :], func=ACT.Exp, bias=ment_col[:, d : d + 1])
+
+        def sum_all(h):
+            order = [D] + list(range(D))
+            for i, d in enumerate(order):
+                nc.tensor.matmul(tot[h], ex[h][:, d, :], ident[:], start=(i == 0), stop=(i == D), is_transpose=True)
+
+        def sum_gold(h):
+            for d in range(D):
+                nc.vector.tensor_scalar(eg[h][:, d, :], ex[h][:, d, :], gold_col[:, d : d + 1], EPS if d == 0 else 0.0, ALU.mult, ALU.add)
+            for d in range(D):
+                nc.tensor.matmul(den[h], eg[h][:, d, :], ident[:], start=(d == 0), stop=(d == D - 1), is_transpose=True)
+
+        relu_low(0)
+        pair_max(0, 0)
+        pair_max(0, 1)
+        relu_low(1)
+        top_max(0)
+        pair_max(1, 0)
+        exps(0, 0, 2)
+        pair_max(1, 1)
+        exps(0, 2, 2)
+        top_max(1)
+        sum_all(0)
+        exps(1, 0, 2)
+        exps(1, 2, 1)
+        exps(1, 3, 1)
+        sum_gold(0)
+        sum_all(1)
+        sum_gold(1)
+
+        logs = [diff[1][:, 2:4, :], diff[1][:, 0:2, :]]
+        nc.scalar.activation(out=logs[0][:, 1, :], in_=tot[0], func=ACT.Ln)
+        nc.scalar.activation(out=logs[0][:, 0, :], in_=den[0], func=ACT.Ln)
+        nc.scalar.activation(out=logs[1][:, 1, :], in_=tot[1], func=ACT.Ln)
+        nc.scalar.activation(out=logs[1][:, 0, :], in_=den[1], func=ACT.Ln)
+        for h in range(HALVES):
+            res = sb.tile([P, G], F32, name="res%d" % h)
+            nc.vector.tensor_tensor(res[:], logs[h][:, 1, :], logs[h][:, 0, :], ALU.subtract)
+            nc.sync.dma_start(out=out[h * P : (h + 1) * P, :], in_=res[:])

@@ -23,6 +23,7 @@ G = S // D
 HALVES = V // P
 PAIRS = D // 2
 EPS = 0.001
+FILL = 64
 
 
 def tile_picked_ycoref_loss_p_kernel(tc, x_words, x_scales, hT, ment, gold, offs, out):
@@ -35,15 +36,17 @@ def tile_picked_ycoref_loss_p_kernel(tc, x_words, x_scales, hT, ment, gold, offs
         ment_win = sb.tile([P, T], F32, name="ment_win")
         word_win = [sb.tile([P, T], U32, name="word_win%d" % o) for o in range(PASSES)]
         scale_win = sb.tile([P, T], U8, name="scale_win")
-        h_raw = [sb.tile([P, PACK, V], F32, name="h_raw%d" % o) for o in range(PASSES)]
+        h_first = sb.tile([P, PACK, V], F32, name="h_first")
+        h_last = [sb.tile([P, PACK, P], F32, name="h_last%d" % h) for h in range(HALVES)]
+        h_raw = [[h_first[:, :, h * P : (h + 1) * P] for h in range(HALVES)], [h_last[h][:] for h in range(HALVES)]]
         gold_col = sb.tile([P, D], F32, name="gold_col")
         ident = sb.tile([P, P], F32, name="ident")
 
         zero_col = sb.tile([P, 1], F32, name="zero_col")
-        nc.gpsimd.memset(scale_win[:].bitcast(I32), 0)
+        nc.vector.memset(scale_win[:].bitcast(I32), 0)
         nc.gpsimd.memset(zero_col[:], 0.0)
+        nc.vector.memset(ment_win[0 : P - 1, FILL:], 0.0)
         make_identity(nc, ident[:])
-        nc.scalar.activation(out=ment_win[0 : P - 1, :], in_=zero_col[0 : P - 1, :].to_broadcast([P - 1, T]), func=ACT.Copy)
 
         def load_words(o):
             nc.sync.dma_start(
@@ -51,43 +54,52 @@ def tile_picked_ycoref_loss_p_kernel(tc, x_words, x_scales, hT, ment, gold, offs
                 in_=x_words[o].rearrange("p n t -> p (n t)").bitcast(I32),
             )
 
-        def load_h(o):
-            rows = hT[o * P * PACK : (o + 1) * P * PACK, :]
-            nc.sync.dma_start(out=h_raw[o][:], in_=rows.rearrange("(p j) w -> p j w", j=PACK))
+        h_rows = hT.rearrange("(o p j) w -> o p j w", p=P, j=PACK)
 
+        load_words(0)
         nc.sync.dma_start(offsets[:], offs)
         nc.sync.dma_start(out=ment_win[P - 1 : P, :], in_=ment[0:1, :])
-        load_words(0)
         for q in range(4):
             nc.sync.dma_start(
                 out=scale_win[32 * q : 32 * q + 4 * PASSES, :].bitcast(I32),
                 in_=x_scales[:, 4 * q : 4 * q + 4, :].bitcast(I32),
             )
-        load_h(0)
+        nc.scalar.activation(out=ment_win[0 : P - 1, :FILL], in_=zero_col[0 : P - 1, :].to_broadcast([P - 1, FILL]), func=ACT.Copy)
+        nc.sync.dma_start(out=h_first[:], in_=h_rows[0])
         load_words(1)
-        load_h(1)
+        for h in range(HALVES):
+            nc.sync.dma_start(out=h_last[h][:], in_=h_rows[1][:, :, h * P : (h + 1) * P])
         nc.sync.dma_start(out=gold_col[:], in_=gold[0:1, :].rearrange("o (g d) -> (o g) d", d=D))
 
         ment_row = sb.tile([P, S], F32, name="ment_row")
         nc.scalar.activation(out=ment_row[:], in_=ment_win[:].indirect(offsets[:]), func=ACT.Copy)
-        ment_ps = ps.tile([P, D, P], F32, name="ment_ps")
+        ment_ps = ps.tile([P, D, P], F32, name="ment_ps", tag="shared")
         for d in range(D):
             nc.tensor.transpose(ment_ps[:, d, :], ment_row[:].rearrange("p (g d) -> p d g", d=D)[:, d, :], ident[:])
-        ment_col = sb.tile([P, D], F32, name="ment_col")
-        nc.scalar.copy(out=ment_col[:], in_=ment_ps[:, :, P - 1])
+        ment_col = h_first[:, 0, P : P + D]
 
         x_code = [sb.tile([P, D, G], U32, name="x_code%d" % o, align_bytes=64) for o in range(PASSES)]
         x_scale = sb.tile([P, D, G], U8, name="x_scale", align_bytes=64)
         h_bf = [[sb.tile([P, P, PACK], BF16, name="h_bf%d%d" % (o, h), align_bytes=64) for h in range(HALVES)] for o in range(PASSES)]
         h_code = [[sb.tile([P, P], U32, name="h_code%d%d" % (o, h), align_bytes=64) for h in range(HALVES)] for o in range(PASSES)]
         h_scale = [[sb.tile([P, P], U8, name="h_scale%d%d" % (o, h), align_bytes=64) for h in range(HALVES)] for o in range(PASSES)]
-        score = [[ps.tile([P, 2, P], F32, name="score%d%d" % (h, r)) for r in range(PAIRS)] for h in range(HALVES)]
+        banks = [[(0,), (1,), (2, 3)], [(0, 1), (2, 3)]]
+        score = [{}, {}]
+        for h in range(HALVES):
+            for run in banks[h]:
+                bank = ps.tile([P, len(run), P], F32, name="score%d%d" % (h, run[0]))
+                for i, d in enumerate(run):
+                    score[h][d] = (bank, i, len(run))
+
+        def scores(h, d0, n):
+            bank, i, size = score[h][d0]
+            return bank[:, i : i + n, :]
 
         def gather_words(o):
             nc.vector.tensor_copy(out=x_code[o][:].rearrange("p d g -> p g d"), in_=word_win[o][:].indirect(offsets[:]))
 
         def cast(copy, o, h):
-            copy(out=h_bf[o][h][:], in_=h_raw[o][:, :, h * P : (h + 1) * P].rearrange("p j w -> p w j"))
+            copy(out=h_bf[o][h][:], in_=h_raw[o][h].rearrange("p j w -> p w j"))
 
         def quant(o, h):
             nc.vector.quantize_mx(
@@ -97,34 +109,35 @@ def tile_picked_ycoref_loss_p_kernel(tc, x_words, x_scales, hT, ment, gold, offs
         def product(o, h):
             for d in range(D):
                 nc.tensor.matmul_mx(
-                    out=score[h][d // 2][:, d % 2, :],
+                    out=scores(h, d, 1)[:, 0, :],
                     lhsT=x_code[o][:, d, :].bitcast(FP8X4),
                     lhsT_scale=x_scale[4 * o : P, d, :],
                     rhs=h_code[o][h][:].bitcast(FP8X4),
                     rhs_scale=h_scale[o][h][:],
-                    start=(o == 0 and d % 2 == 0),
-                    stop=(o == PASSES - 1 and d % 2 == 1),
+                    start=(o == 0 and score[h][d][1] == 0),
+                    stop=(o == PASSES - 1 and score[h][d][1] == score[h][d][2] - 1),
                 )
 
         gather_words(0)
         nc.vector.tensor_copy(out=x_scale[:].rearrange("p d g -> p g d"), in_=scale_win[:].indirect(offsets[:]))
         cast(nc.scalar.copy, 0, 0)
         cast(nc.scalar.copy, 0, 1)
-        gather_words(1)
+        nc.scalar.copy(out=ment_col, in_=ment_ps[:, :, P - 1])
         quant(0, 0)
         product(0, 0)
+        gather_words(1)
         cast(nc.vector.tensor_copy, 1, 0)
-        cast(nc.scalar.copy, 1, 1)
         quant(0, 1)
         product(0, 1)
         quant(1, 0)
         product(1, 0)
+        cast(nc.vector.tensor_copy, 1, 1)
         quant(1, 1)
         product(1, 1)
 
         ex = [sb.tile([P, D + 1, P], F32, name="ex%d" % h) for h in range(HALVES)]
         eg = [sb.tile([P, D, P], F32, name="eg%d" % h) for h in range(HALVES)]
-        tot0 = ps.tile([P, G], F32, name="tot0")
+        tot0 = ps.tile([P, G], F32, name="tot0", tag="shared")
         den0 = ps.tile([P, G], F32, name="den0")
         sums1 = ps.tile([P, 2, G], F32, name="sums1")
         tot = [tot0[:], sums1[:, 0, :]]
@@ -137,11 +150,11 @@ def tile_picked_ycoref_loss_p_kernel(tc, x_words, x_scales, hT, ment, gold, offs
 
         def relu_low(h):
             for d in range(2):
-                nc.scalar.activation(out=low[h][:, d, :], in_=score[h][0][:, d, :], func=ACT.Relu, bias=ment_col[:, d : d + 1])
+                nc.scalar.activation(out=low[h][:, d, :], in_=scores(h, d, 1)[:, 0, :], func=ACT.Relu, bias=ment_col[:, d : d + 1])
 
         def pair_max(h, i):
             nc.vector.scalar_tensor_tensor(
-                pair[h][:, i, :], score[h][1][:, i, :], ment_col[:, 2 + i : 3 + i], low[h][:, i, :], ALU.add, ALU.max
+                pair[h][:, i, :], scores(h, 2 + i, 1)[:, 0, :], ment_col[:, 2 + i : 3 + i], low[h][:, i, :], ALU.add, ALU.max
             )
 
         def top_max(h):
@@ -151,7 +164,7 @@ def tile_picked_ycoref_loss_p_kernel(tc, x_words, x_scales, hT, ment, gold, offs
         def exps(h, d0, n):
             nc.vector.tensor_tensor(
                 diff[h][:, d0 : d0 + n, :],
-                score[h][d0 // 2][:, d0 % 2 : d0 % 2 + n, :],
+                scores(h, d0, n),
                 top[h][:].unsqueeze(1).to_broadcast([P, n, P]),
                 ALU.subtract,
             )
@@ -175,10 +188,11 @@ def tile_picked_ycoref_loss_p_kernel(tc, x_words, x_scales, hT, ment, gold, offs
         relu_low(1)
         top_max(0)
         pair_max(1, 0)
-        exps(0, 0, 2)
         pair_max(1, 1)
-        exps(0, 2, 2)
+        exps(0, 0, 1)
+        exps(0, 1, 1)
         top_max(1)
+        exps(0, 2, 2)
         sum_all(0)
         exps(1, 0, 2)
         exps(1, 2, 1)

@@ -37,8 +37,8 @@ def tile_picked_ycoref_loss_p_kernel(tc, x_words, x_scales, hT, ment, gold, offs
         word_win = [sb.tile([P, T], U32, name="word_win%d" % o) for o in range(PASSES)]
         scale_win = sb.tile([P, T], U8, name="scale_win")
         h_first = sb.tile([P, PACK, V], F32, name="h_first")
-        h_last = [sb.tile([P, PACK, P], F32, name="h_last%d" % h) for h in range(HALVES)]
-        h_raw = [[h_first[:, :, h * P : (h + 1) * P] for h in range(HALVES)], [h_last[h][:] for h in range(HALVES)]]
+        h_last = sb.tile([P, PACK, V], F32, name="h_last")
+        h_raw = [[tile[:, :, h * P : (h + 1) * P] for h in range(HALVES)] for tile in (h_first, h_last)]
         gold_col = sb.tile([P, D], F32, name="gold_col")
         ident = sb.tile([P, P], F32, name="ident")
 
@@ -66,9 +66,8 @@ def tile_picked_ycoref_loss_p_kernel(tc, x_words, x_scales, hT, ment, gold, offs
             )
         nc.scalar.activation(out=ment_win[0 : P - 1, :FILL], in_=zero_col[0 : P - 1, :].to_broadcast([P - 1, FILL]), func=ACT.Copy)
         nc.sync.dma_start(out=h_first[:], in_=h_rows[0])
+        nc.sync.dma_start(out=h_last[:], in_=h_rows[1])
         load_words(1)
-        for h in range(HALVES):
-            nc.sync.dma_start(out=h_last[h][:], in_=h_rows[1][:, :, h * P : (h + 1) * P])
         nc.sync.dma_start(out=gold_col[:], in_=gold[0:1, :].rearrange("o (g d) -> (o g) d", d=D))
 
         ment_row = sb.tile([P, S], F32, name="ment_row")
@@ -76,7 +75,7 @@ def tile_picked_ycoref_loss_p_kernel(tc, x_words, x_scales, hT, ment, gold, offs
         ment_ps = ps.tile([P, D, P], F32, name="ment_ps", tag="shared")
         for d in range(D):
             nc.tensor.transpose(ment_ps[:, d, :], ment_row[:].rearrange("p (g d) -> p d g", d=D)[:, d, :], ident[:])
-        ment_col = h_first[:, 0, P : P + D]
+        ment_col = h_last[:, 0, P : P + D]
 
         x_code = [sb.tile([P, D, G], U32, name="x_code%d" % o, align_bytes=64) for o in range(PASSES)]
         x_scale = sb.tile([P, D, G], U8, name="x_scale", align_bytes=64)
@@ -106,8 +105,8 @@ def tile_picked_ycoref_loss_p_kernel(tc, x_words, x_scales, hT, ment, gold, offs
                 out=h_code[o][h][:].bitcast(FP8X4), scales=h_scale[o][h][:], in_=h_bf[o][h][:].rearrange("p w j -> p (w j)")
             )
 
-        def product(o, h):
-            for d in range(D):
+        def product(o, h, ds):
+            for d in ds:
                 nc.tensor.matmul_mx(
                     out=scores(h, d, 1)[:, 0, :],
                     lhsT=x_code[o][:, d, :].bitcast(FP8X4),
@@ -121,32 +120,34 @@ def tile_picked_ycoref_loss_p_kernel(tc, x_words, x_scales, hT, ment, gold, offs
         gather_words(0)
         nc.vector.tensor_copy(out=x_scale[:].rearrange("p d g -> p g d"), in_=scale_win[:].indirect(offsets[:]))
         cast(nc.scalar.copy, 0, 0)
-        cast(nc.scalar.copy, 0, 1)
-        nc.scalar.copy(out=ment_col, in_=ment_ps[:, :, P - 1])
+        cast(nc.vector.tensor_copy, 0, 1)
         quant(0, 0)
-        product(0, 0)
-        gather_words(1)
-        cast(nc.vector.tensor_copy, 1, 0)
         quant(0, 1)
-        product(0, 1)
+        product(0, 0, range(D))
+        product(0, 1, range(D))
+        cast(nc.scalar.copy, 1, 0)
+        cast(nc.scalar.copy, 1, 1)
+        nc.scalar.copy(out=ment_col, in_=ment_ps[:, :, P - 1])
         quant(1, 0)
-        product(1, 0)
-        cast(nc.vector.tensor_copy, 1, 1)
+        gather_words(1)
         quant(1, 1)
-        product(1, 1)
+        for ds in ((0, 1), (2, 3)):
+            for h in range(HALVES):
+                product(1, h, ds)
 
         ex = [sb.tile([P, D + 1, P], F32, name="ex%d" % h) for h in range(HALVES)]
         eg = [sb.tile([P, D, P], F32, name="eg%d" % h) for h in range(HALVES)]
         tot0 = ps.tile([P, G], F32, name="tot0", tag="shared")
         den0 = ps.tile([P, G], F32, name="den0")
         sums1 = ps.tile([P, 2, G], F32, name="sums1")
-        tot = [tot0[:], sums1[:, 0, :]]
-        den = [den0[:], sums1[:, 1, :]]
+        tot = [tot0[:], sums1[:, 1, :]]
+        den = [den0[:], sums1[:, 0, :]]
 
         diff = [sb.tile([P, D, P], F32, name="diff%d" % h) for h in range(HALVES)]
         low = [sb.tile([P, 2, P], F32, name="low%d" % h) for h in range(HALVES)]
         pair = [sb.tile([P, 2, P], F32, name="pair%d" % h) for h in range(HALVES)]
-        top = [sb.tile([P, P], F32, name="top%d" % h) for h in range(HALVES)]
+        top0 = sb.tile([P, P], F32, name="top0")
+        top = [top0[:], eg[0][:, D - 1, :]]
 
         def relu_low(h):
             for d in range(2):
@@ -158,14 +159,14 @@ def tile_picked_ycoref_loss_p_kernel(tc, x_words, x_scales, hT, ment, gold, offs
             )
 
         def top_max(h):
-            nc.vector.tensor_tensor(top[h][:], pair[h][:, 0, :], pair[h][:, 1, :], ALU.max)
-            nc.scalar.activation(out=ex[h][:, D, :], in_=top[h][:], func=ACT.Exp, scale=-1.0)
+            nc.vector.tensor_tensor(top[h], pair[h][:, 0, :], pair[h][:, 1, :], ALU.max)
+            nc.scalar.activation(out=ex[h][:, D, :], in_=top[h], func=ACT.Exp, scale=-1.0)
 
         def exps(h, d0, n):
             nc.vector.tensor_tensor(
                 diff[h][:, d0 : d0 + n, :],
                 scores(h, d0, n),
-                top[h][:].unsqueeze(1).to_broadcast([P, n, P]),
+                top[h].unsqueeze(1).to_broadcast([P, n, P]),
                 ALU.subtract,
             )
             for d in range(d0, d0 + n):
@@ -178,34 +179,33 @@ def tile_picked_ycoref_loss_p_kernel(tc, x_words, x_scales, hT, ment, gold, offs
 
         def sum_gold(h):
             for d in range(D):
-                nc.vector.tensor_scalar(eg[h][:, d, :], ex[h][:, d, :], gold_col[:, d : d + 1], EPS if d == 0 else 0.0, ALU.mult, ALU.add)
-            for d in range(D):
                 nc.tensor.matmul(den[h], eg[h][:, d, :], ident[:], start=(d == 0), stop=(d == D - 1), is_transpose=True)
 
-        relu_low(0)
-        pair_max(0, 0)
-        pair_max(0, 1)
-        relu_low(1)
-        top_max(0)
-        pair_max(1, 0)
-        pair_max(1, 1)
+        for h in range(HALVES):
+            relu_low(h)
+        for h in range(HALVES):
+            pair_max(h, 0)
+            pair_max(h, 1)
+        for h in range(HALVES):
+            top_max(h)
         exps(0, 0, 1)
         exps(0, 1, 1)
-        top_max(1)
         exps(0, 2, 2)
         sum_all(0)
         exps(1, 0, 2)
         exps(1, 2, 1)
         exps(1, 3, 1)
+        nc.vector.tensor_tensor(eg[0][:], ex[0][:, 0:D, :], gold_col[:].unsqueeze(2).to_broadcast([P, D, P]), ALU.mult)
         sum_gold(0)
         sum_all(1)
+        for d in range(D):
+            nc.vector.tensor_scalar(eg[1][:, d, :], ex[1][:, d, :], gold_col[:, d : d + 1], EPS if d == 0 else 0.0, ALU.mult, ALU.add)
         sum_gold(1)
 
         logs = [diff[1][:, 2:4, :], diff[1][:, 0:2, :]]
         nc.scalar.activation(out=logs[0][:, 1, :], in_=tot[0], func=ACT.Ln)
-        nc.scalar.activation(out=logs[0][:, 0, :], in_=den[0], func=ACT.Ln)
-        nc.scalar.activation(out=logs[1][:, 1, :], in_=tot[1], func=ACT.Ln)
-        nc.scalar.activation(out=logs[1][:, 0, :], in_=den[1], func=ACT.Ln)
+        nc.scalar.activation(out=logs[0][:, 0, :], in_=den[0], func=ACT.Ln, bias=EPS)
+        nc.scalar.activation(out=logs[1], in_=sums1[:], func=ACT.Ln)
         for h in range(HALVES):
             res = sb.tile([P, G], F32, name="res%d" % h)
             nc.vector.tensor_tensor(res[:], logs[h][:, 1, :], logs[h][:, 0, :], ALU.subtract)

@@ -21,9 +21,11 @@ PACK = 4
 PASSES = K // (P * PACK)
 G = S // D
 HALVES = V // P
-PAIRS = D // 2
+QUADRANT = 32
+SCALE_ROWS = 4
+LIST_GROUP = 16
+PAIRS = ((0, 1), (2, 3))
 EPS = 0.001
-FILL = 64
 
 
 def tile_picked_ycoref_loss_p_kernel(tc, x_words, x_scales, hT, ment, gold, offs, out):
@@ -32,20 +34,17 @@ def tile_picked_ycoref_loss_p_kernel(tc, x_words, x_scales, hT, ment, gold, offs
         sb = ctx.enter_context(tc.tile_pool(name="sb", bufs=1))
         ps = ctx.enter_context(tc.psum_pool(name="ps", bufs=1))
 
-        offsets = sb.tile([P, S // 16], U16, name="offsets")
+        offsets = sb.tile([P, S // LIST_GROUP], U16, name="offsets")
         ment_win = sb.tile([P, T], F32, name="ment_win")
         word_win = [sb.tile([P, T], U32, name="word_win%d" % o) for o in range(PASSES)]
         scale_win = sb.tile([P, T], U8, name="scale_win")
-        h_first = sb.tile([P, PACK, V], F32, name="h_first")
-        h_last = sb.tile([P, PACK, V], F32, name="h_last")
-        h_raw = [[tile[:, :, h * P : (h + 1) * P] for h in range(HALVES)] for tile in (h_first, h_last)]
+        h_raw = [sb.tile([P, PACK, V], F32, name="h_raw%d" % o) for o in range(PASSES)]
         gold_col = sb.tile([P, D], F32, name="gold_col")
         ident = sb.tile([P, P], F32, name="ident")
-
         zero_col = sb.tile([P, 1], F32, name="zero_col")
+
         nc.vector.memset(scale_win[:].bitcast(I32), 0)
         nc.gpsimd.memset(zero_col[:], 0.0)
-        nc.vector.memset(ment_win[0 : P - 1, FILL:], 0.0)
         make_identity(nc, ident[:])
 
         def load_words(o):
@@ -59,148 +58,137 @@ def tile_picked_ycoref_loss_p_kernel(tc, x_words, x_scales, hT, ment, gold, offs
         load_words(0)
         nc.sync.dma_start(offsets[:], offs)
         nc.sync.dma_start(out=ment_win[P - 1 : P, :], in_=ment[0:1, :])
-        for q in range(4):
+        for q in range(P // QUADRANT):
             nc.sync.dma_start(
-                out=scale_win[32 * q : 32 * q + 4 * PASSES, :].bitcast(I32),
-                in_=x_scales[:, 4 * q : 4 * q + 4, :].bitcast(I32),
+                out=scale_win[QUADRANT * q : QUADRANT * q + SCALE_ROWS * PASSES, :].bitcast(I32),
+                in_=x_scales[:, SCALE_ROWS * q : SCALE_ROWS * (q + 1), :].bitcast(I32),
             )
-        nc.scalar.activation(out=ment_win[0 : P - 1, :FILL], in_=zero_col[0 : P - 1, :].to_broadcast([P - 1, FILL]), func=ACT.Copy)
-        nc.sync.dma_start(out=h_first[:], in_=h_rows[0])
-        nc.sync.dma_start(out=h_last[:], in_=h_rows[1])
+        nc.scalar.activation(
+            out=ment_win[0 : P - 1, :], in_=zero_col[0 : P - 1, :].to_broadcast([P - 1, T]), func=ACT.Copy
+        )
+        for o in range(PASSES):
+            nc.sync.dma_start(out=h_raw[o][:], in_=h_rows[o])
         load_words(1)
         nc.sync.dma_start(out=gold_col[:], in_=gold[0:1, :].rearrange("o (g d) -> (o g) d", d=D))
 
         ment_row = sb.tile([P, S], F32, name="ment_row")
         nc.scalar.activation(out=ment_row[:], in_=ment_win[:].indirect(offsets[:]), func=ACT.Copy)
-        ment_ps = ps.tile([P, D, P], F32, name="ment_ps", tag="shared")
+        ment_ps = ps.tile([P, D, P], F32, name="ment_ps")
         for d in range(D):
             nc.tensor.transpose(ment_ps[:, d, :], ment_row[:].rearrange("p (g d) -> p d g", d=D)[:, d, :], ident[:])
-        ment_col = h_last[:, 0, P : P + D]
+        ment_col = h_raw[PASSES - 1][:, 0, P : P + D]
 
         x_code = [sb.tile([P, D, G], U32, name="x_code%d" % o, align_bytes=64) for o in range(PASSES)]
         x_scale = sb.tile([P, D, G], U8, name="x_scale", align_bytes=64)
-        h_bf = [[sb.tile([P, P, PACK], BF16, name="h_bf%d%d" % (o, h), align_bytes=64) for h in range(HALVES)] for o in range(PASSES)]
-        h_code = [[sb.tile([P, P], U32, name="h_code%d%d" % (o, h), align_bytes=64) for h in range(HALVES)] for o in range(PASSES)]
-        h_scale = [[sb.tile([P, P], U8, name="h_scale%d%d" % (o, h), align_bytes=64) for h in range(HALVES)] for o in range(PASSES)]
-        banks = [[(0,), (1,), (2, 3)], [(0, 1), (2, 3)]]
-        score = [{}, {}]
-        for h in range(HALVES):
-            for run in banks[h]:
-                bank = ps.tile([P, len(run), P], F32, name="score%d%d" % (h, run[0]))
-                for i, d in enumerate(run):
-                    score[h][d] = (bank, i, len(run))
 
-        def scores(h, d0, n):
-            bank, i, size = score[h][d0]
-            return bank[:, i : i + n, :]
+        def h_tiles(shape, dtype, name):
+            return [
+                [sb.tile(shape, dtype, name="%s%d%d" % (name, o, h), align_bytes=64) for h in range(HALVES)]
+                for o in range(PASSES)
+            ]
 
-        def gather_words(o):
-            nc.vector.tensor_copy(out=x_code[o][:].rearrange("p d g -> p g d"), in_=word_win[o][:].indirect(offsets[:]))
+        h_bf = h_tiles([P, P, PACK], BF16, "h_bf")
+        h_code = h_tiles([P, P], U32, "h_code")
+        h_scale = h_tiles([P, P], U8, "h_scale")
+        banks = [[ps.tile([P, 2, P], F32, name="score%d%d" % (h, r)) for r in range(len(PAIRS))] for h in range(HALVES)]
 
-        def cast(copy, o, h):
-            copy(out=h_bf[o][h][:], in_=h_raw[o][h].rearrange("p j w -> p w j"))
+        def score(h, d):
+            return banks[h][d // 2][:, d % 2, :]
 
-        def quant(o, h):
+        def gather(dst, window):
+            nc.vector.tensor_copy(out=dst[:].rearrange("p d g -> p g d"), in_=window[:].indirect(offsets[:]))
+
+        def round_h(copy, o, h):
+            copy(out=h_bf[o][h][:], in_=h_raw[o][:, :, h * P : (h + 1) * P].rearrange("p j w -> p w j"))
+
+        def quantise(o, h):
             nc.vector.quantize_mx(
-                out=h_code[o][h][:].bitcast(FP8X4), scales=h_scale[o][h][:], in_=h_bf[o][h][:].rearrange("p w j -> p (w j)")
+                out=h_code[o][h][:].bitcast(FP8X4),
+                scales=h_scale[o][h][:],
+                in_=h_bf[o][h][:].rearrange("p w j -> p (w j)"),
             )
 
-        def product(o, h, ds):
-            for d in ds:
+        def product(o, h, members):
+            for d in members:
                 nc.tensor.matmul_mx(
-                    out=scores(h, d, 1)[:, 0, :],
+                    out=score(h, d),
                     lhsT=x_code[o][:, d, :].bitcast(FP8X4),
-                    lhsT_scale=x_scale[4 * o : P, d, :],
+                    lhsT_scale=x_scale[SCALE_ROWS * o : P, d, :],
                     rhs=h_code[o][h][:].bitcast(FP8X4),
                     rhs_scale=h_scale[o][h][:],
-                    start=(o == 0 and score[h][d][1] == 0),
-                    stop=(o == PASSES - 1 and score[h][d][1] == score[h][d][2] - 1),
+                    start=(o == 0 and d % 2 == 0),
+                    stop=(o == PASSES - 1 and d % 2 == 1),
                 )
 
-        gather_words(0)
-        nc.vector.tensor_copy(out=x_scale[:].rearrange("p d g -> p g d"), in_=scale_win[:].indirect(offsets[:]))
-        cast(nc.scalar.copy, 0, 0)
-        cast(nc.vector.tensor_copy, 0, 1)
-        quant(0, 0)
-        quant(0, 1)
-        product(0, 0, range(D))
-        product(0, 1, range(D))
-        cast(nc.scalar.copy, 1, 0)
-        cast(nc.scalar.copy, 1, 1)
+        gather(x_code[0], word_win[0])
+        gather(x_scale, scale_win)
+        round_h(nc.scalar.copy, 0, 0)
+        round_h(nc.vector.tensor_copy, 0, 1)
+        for h in range(HALVES):
+            quantise(0, h)
+        for h in range(HALVES):
+            product(0, h, range(D))
+        for h in range(HALVES):
+            round_h(nc.scalar.copy, 1, h)
         nc.scalar.copy(out=ment_col, in_=ment_ps[:, :, P - 1])
-        quant(1, 0)
-        gather_words(1)
-        quant(1, 1)
-        for ds in ((0, 1), (2, 3)):
+        quantise(1, 0)
+        gather(x_code[1], word_win[1])
+        quantise(1, 1)
+        for members in PAIRS:
             for h in range(HALVES):
-                product(1, h, ds)
+                product(1, h, members)
 
         ex = [sb.tile([P, D + 1, P], F32, name="ex%d" % h) for h in range(HALVES)]
         eg = [sb.tile([P, D, P], F32, name="eg%d" % h) for h in range(HALVES)]
-        tot0 = ps.tile([P, G], F32, name="tot0", tag="shared")
-        den0 = ps.tile([P, G], F32, name="den0")
-        sums1 = ps.tile([P, 2, G], F32, name="sums1")
-        tot = [tot0[:], sums1[:, 1, :]]
-        den = [den0[:], sums1[:, 0, :]]
-
         diff = [sb.tile([P, D, P], F32, name="diff%d" % h) for h in range(HALVES)]
         low = [sb.tile([P, 2, P], F32, name="low%d" % h) for h in range(HALVES)]
         pair = [sb.tile([P, 2, P], F32, name="pair%d" % h) for h in range(HALVES)]
         top0 = sb.tile([P, P], F32, name="top0")
         top = [top0[:], eg[0][:, D - 1, :]]
 
-        def relu_low(h):
-            for d in range(2):
-                nc.scalar.activation(out=low[h][:, d, :], in_=scores(h, d, 1)[:, 0, :], func=ACT.Relu, bias=ment_col[:, d : d + 1])
-
-        def pair_max(h, i):
-            nc.vector.scalar_tensor_tensor(
-                pair[h][:, i, :], scores(h, 2 + i, 1)[:, 0, :], ment_col[:, 2 + i : 3 + i], low[h][:, i, :], ALU.add, ALU.max
-            )
-
-        def top_max(h):
+        for h in range(HALVES):
+            for i in PAIRS[0]:
+                nc.scalar.activation(out=low[h][:, i, :], in_=score(h, i), func=ACT.Relu, bias=ment_col[:, i : i + 1])
+        for h in range(HALVES):
+            for i, d in enumerate(PAIRS[1]):
+                nc.vector.scalar_tensor_tensor(
+                    pair[h][:, i, :], score(h, d), ment_col[:, d : d + 1], low[h][:, i, :], ALU.add, ALU.max
+                )
+        for h in range(HALVES):
             nc.vector.tensor_tensor(top[h], pair[h][:, 0, :], pair[h][:, 1, :], ALU.max)
             nc.scalar.activation(out=ex[h][:, D, :], in_=top[h], func=ACT.Exp, scale=-1.0)
 
-        def exps(h, d0, n):
-            nc.vector.tensor_tensor(
-                diff[h][:, d0 : d0 + n, :],
-                scores(h, d0, n),
-                top[h].unsqueeze(1).to_broadcast([P, n, P]),
-                ALU.subtract,
-            )
-            for d in range(d0, d0 + n):
-                nc.scalar.activation(out=ex[h][:, d, :], in_=diff[h][:, d, :], func=ACT.Exp, bias=ment_col[:, d : d + 1])
-
-        def sum_all(h):
-            order = [D] + list(range(D))
-            for i, d in enumerate(order):
-                nc.tensor.matmul(tot[h], ex[h][:, d, :], ident[:], start=(i == 0), stop=(i == D), is_transpose=True)
-
-        def sum_gold(h):
+        def exponentials(h):
             for d in range(D):
-                nc.tensor.matmul(den[h], eg[h][:, d, :], ident[:], start=(d == 0), stop=(d == D - 1), is_transpose=True)
+                nc.vector.tensor_tensor(diff[h][:, d, :], score(h, d), top[h], ALU.subtract)
+                nc.scalar.activation(
+                    out=ex[h][:, d, :], in_=diff[h][:, d, :], func=ACT.Exp, bias=ment_col[:, d : d + 1]
+                )
 
-        for h in range(HALVES):
-            relu_low(h)
-        for h in range(HALVES):
-            pair_max(h, 0)
-            pair_max(h, 1)
-        for h in range(HALVES):
-            top_max(h)
-        exps(0, 0, 1)
-        exps(0, 1, 1)
-        exps(0, 2, 2)
-        sum_all(0)
-        exps(1, 0, 2)
-        exps(1, 2, 1)
-        exps(1, 3, 1)
+        tot0 = ps.tile([P, G], F32, name="tot0")
+        den0 = ps.tile([P, G], F32, name="den0")
+        sums1 = ps.tile([P, 2, G], F32, name="sums1")
+        tot = [tot0[:], sums1[:, 1, :]]
+        den = [den0[:], sums1[:, 0, :]]
+
+        def add_transposed(dst, src, slots):
+            for i, slot in enumerate(slots):
+                nc.tensor.matmul(
+                    dst, src[:, slot, :], ident[:], start=(i == 0), stop=(i == len(slots) - 1), is_transpose=True
+                )
+
+        total_slots = [D] + list(range(D))
+        exponentials(0)
+        add_transposed(tot[0], ex[0], total_slots)
+        exponentials(1)
         nc.vector.tensor_tensor(eg[0][:], ex[0][:, 0:D, :], gold_col[:].unsqueeze(2).to_broadcast([P, D, P]), ALU.mult)
-        sum_gold(0)
-        sum_all(1)
+        add_transposed(den[0], eg[0], range(D))
+        add_transposed(tot[1], ex[1], total_slots)
         for d in range(D):
-            nc.vector.tensor_scalar(eg[1][:, d, :], ex[1][:, d, :], gold_col[:, d : d + 1], EPS if d == 0 else 0.0, ALU.mult, ALU.add)
-        sum_gold(1)
+            nc.vector.tensor_scalar(
+                eg[1][:, d, :], ex[1][:, d, :], gold_col[:, d : d + 1], EPS if d == 0 else 0.0, ALU.mult, ALU.add
+            )
+        add_transposed(den[1], eg[1], range(D))
 
         logs = [diff[1][:, 2:4, :], diff[1][:, 0:2, :]]
         nc.scalar.activation(out=logs[0][:, 1, :], in_=tot[0], func=ACT.Ln)

from contextlib import ExitStack

import concourse.mybir as mybir
from concourse.masks import make_identity

K, T, S, V, D = 1024, 1024, 512, 256, 4
FLOPS = 2 * K * S * V

F32 = mybir.dt.float32
BF16 = mybir.dt.bfloat16
I32 = mybir.dt.int32
U32 = mybir.dt.uint32
U16 = mybir.dt.uint16
U8 = mybir.dt.uint8
FP8X4 = mybir.dt.float8_e4m3fn_x4
ALU = mybir.AluOpType
ACT = mybir.ActivationFunctionType

P = 128
PACK = 4
PASSES = K // (P * PACK)
G = S // D
HALVES = V // P
QUADRANT = 32
SCALE_ROWS = 4
LIST_GROUP = 16
PAIRS = ((0, 1), (2, 3))
EPS = 0.001


def tile_picked_ycoref_loss_p_kernel(tc, x_words, x_scales, hT, ment, gold, offs, out):
    nc = tc.nc
    with ExitStack() as ctx:
        sb = ctx.enter_context(tc.tile_pool(name="sb", bufs=1))
        ps = ctx.enter_context(tc.psum_pool(name="ps", bufs=1))

        offsets = sb.tile([P, S // LIST_GROUP], U16, name="offsets")
        ment_win = sb.tile([P, T], F32, name="ment_win")
        word_win = [sb.tile([P, T], U32, name="word_win%d" % o) for o in range(PASSES)]
        scale_win = sb.tile([P, T], U8, name="scale_win")
        h_raw = [sb.tile([P, PACK, V], F32, name="h_raw%d" % o) for o in range(PASSES)]
        gold_col = sb.tile([P, D], F32, name="gold_col")
        ident = sb.tile([P, P], F32, name="ident")
        zero_col = sb.tile([P, 1], F32, name="zero_col")

        nc.vector.memset(scale_win[:].bitcast(I32), 0)
        nc.gpsimd.memset(zero_col[:], 0.0)
        make_identity(nc, ident[:])

        def load_words(o):
            nc.sync.dma_start(
                out=word_win[o][:].bitcast(I32),
                in_=x_words[o].rearrange("p n t -> p (n t)").bitcast(I32),
            )

        h_rows = hT.rearrange("(o p j) w -> o p j w", p=P, j=PACK)

        load_words(0)
        nc.sync.dma_start(offsets[:], offs)
        nc.sync.dma_start(out=ment_win[P - 1 : P, :], in_=ment[0:1, :])
        for q in range(P // QUADRANT):
            nc.sync.dma_start(
                out=scale_win[QUADRANT * q : QUADRANT * q + SCALE_ROWS * PASSES, :].bitcast(I32),
                in_=x_scales[:, SCALE_ROWS * q : SCALE_ROWS * (q + 1), :].bitcast(I32),
            )
        nc.scalar.activation(
            out=ment_win[0 : P - 1, :], in_=zero_col[0 : P - 1, :].to_broadcast([P - 1, T]), func=ACT.Copy
        )
        for o in range(PASSES):
            nc.sync.dma_start(out=h_raw[o][:], in_=h_rows[o])
        load_words(1)
        nc.sync.dma_start(out=gold_col[:], in_=gold[0:1, :].rearrange("o (g d) -> (o g) d", d=D))

        ment_row = sb.tile([P, S], F32, name="ment_row")
        nc.scalar.activation(out=ment_row[:], in_=ment_win[:].indirect(offsets[:]), func=ACT.Copy)
        ment_ps = ps.tile([P, D, P], F32, name="ment_ps")
        for d in range(D):
            nc.tensor.transpose(ment_ps[:, d, :], ment_row[:].rearrange("p (g d) -> p d g", d=D)[:, d, :], ident[:])
        ment_col = h_raw[PASSES - 1][:, 0, P : P + D]

        x_code = [sb.tile([P, D, G], U32, name="x_code%d" % o, align_bytes=64) for o in range(PASSES)]
        x_scale = sb.tile([P, D, G], U8, name="x_scale", align_bytes=64)

        def h_tiles(shape, dtype, name):
            return [
                [sb.tile(shape, dtype, name="%s%d%d" % (name, o, h), align_bytes=64) for h in range(HALVES)]
                for o in range(PASSES)
            ]

        h_bf = h_tiles([P, P, PACK], BF16, "h_bf")
        h_code = h_tiles([P, P], U32, "h_code")
        h_scale = h_tiles([P, P], U8, "h_scale")
        banks = [[ps.tile([P, 2, P], F32, name="score%d%d" % (h, r)) for r in range(len(PAIRS))] for h in range(HALVES)]

        def score(h, d):
            return banks[h][d // 2][:, d % 2, :]

        def gather(dst, window):
            nc.vector.tensor_copy(out=dst[:].rearrange("p d g -> p g d"), in_=window[:].indirect(offsets[:]))

        def round_h(copy, o, h):
            copy(out=h_bf[o][h][:], in_=h_raw[o][:, :, h * P : (h + 1) * P].rearrange("p j w -> p w j"))

        def quantise(o, h):
            nc.vector.quantize_mx(
                out=h_code[o][h][:].bitcast(FP8X4),
                scales=h_scale[o][h][:],
                in_=h_bf[o][h][:].rearrange("p w j -> p (w j)"),
            )

        def product(o, h, members):
            for d in members:
                nc.tensor.matmul_mx(
                    out=score(h, d),
                    lhsT=x_code[o][:, d, :].bitcast(FP8X4),
                    lhsT_scale=x_scale[SCALE_ROWS * o : P, d, :],
                    rhs=h_code[o][h][:].bitcast(FP8X4),
                    rhs_scale=h_scale[o][h][:],
                    start=(o == 0 and d % 2 == 0),
                    stop=(o == PASSES - 1 and d % 2 == 1),
                )

        gather(x_code[0], word_win[0])
        gather(x_scale, scale_win)
        round_h(nc.scalar.copy, 0, 0)
        round_h(nc.vector.tensor_copy, 0, 1)
        for h in range(HALVES):
            quantise(0, h)
        for h in range(HALVES):
            product(0, h, range(D))
        for h in range(HALVES):
            round_h(nc.scalar.copy, 1, h)
        nc.scalar.copy(out=ment_col, in_=ment_ps[:, :, P - 1])
        quantise(1, 0)
        gather(x_code[1], word_win[1])
        quantise(1, 1)
        for members in PAIRS:
            for h in range(HALVES):
                product(1, h, members)

        ex = [sb.tile([P, D + 1, P], F32, name="ex%d" % h) for h in range(HALVES)]
        eg = [sb.tile([P, D, P], F32, name="eg%d" % h) for h in range(HALVES)]
        diff = [sb.tile([P, D, P], F32, name="diff%d" % h) for h in range(HALVES)]
        low = [sb.tile([P, 2, P], F32, name="low%d" % h) for h in range(HALVES)]
        pair = [sb.tile([P, 2, P], F32, name="pair%d" % h) for h in range(HALVES)]
        top0 = sb.tile([P, P], F32, name="top0")
        top = [top0[:], eg[0][:, D - 1, :]]

        for h in range(HALVES):
            for i in PAIRS[0]:
                nc.scalar.activation(out=low[h][:, i, :], in_=score(h, i), func=ACT.Relu, bias=ment_col[:, i : i + 1])
        for h in range(HALVES):
            for i, d in enumerate(PAIRS[1]):
                nc.vector.scalar_tensor_tensor(
                    pair[h][:, i, :], score(h, d), ment_col[:, d : d + 1], low[h][:, i, :], ALU.add, ALU.max
                )
        for h in range(HALVES):
            nc.vector.tensor_tensor(top[h], pair[h][:, 0, :], pair[h][:, 1, :], ALU.max)
            nc.scalar.activation(out=ex[h][:, D, :], in_=top[h], func=ACT.Exp, scale=-1.0)

        def exponentials(h):
            for d in range(D):
                nc.vector.tensor_tensor(diff[h][:, d, :], score(h, d), top[h], ALU.subtract)
                nc.scalar.activation(
                    out=ex[h][:, d, :], in_=diff[h][:, d, :], func=ACT.Exp, bias=ment_col[:, d : d + 1]
                )

        tot0 = ps.tile([P, G], F32, name="tot0")
        den0 = ps.tile([P, G], F32, name="den0")
        sums1 = ps.tile([P, 2, G], F32, name="sums1")
        tot = [tot0[:], sums1[:, 1, :]]
        den = [den0[:], sums1[:, 0, :]]

        def add_transposed(dst, src, slots):
            for i, slot in enumerate(slots):
                nc.tensor.matmul(
                    dst, src[:, slot, :], ident[:], start=(i == 0), stop=(i == len(slots) - 1), is_transpose=True
                )

        total_slots = [D] + list(range(D))
        exponentials(0)
        add_transposed(tot[0], ex[0], total_slots)
        exponentials(1)
        nc.vector.tensor_tensor(eg[0][:], ex[0][:, 0:D, :], gold_col[:].unsqueeze(2).to_broadcast([P, D, P]), ALU.mult)
        add_transposed(den[0], eg[0], range(D))
        add_transposed(tot[1], ex[1], total_slots)
        for d in range(D):
            nc.vector.tensor_scalar(
                eg[1][:, d, :], ex[1][:, d, :], gold_col[:, d : d + 1], EPS if d == 0 else 0.0, ALU.mult, ALU.add
            )
        add_transposed(den[1], eg[1], range(D))

        logs = [diff[1][:, 2:4, :], diff[1][:, 0:2, :]]
        nc.scalar.activation(out=logs[0][:, 1, :], in_=tot[0], func=ACT.Ln)
        nc.scalar.activation(out=logs[0][:, 0, :], in_=den[0], func=ACT.Ln, bias=EPS)
        nc.scalar.activation(out=logs[1], in_=sums1[:], func=ACT.Ln)
        for h in range(HALVES):
            res = sb.tile([P, G], F32, name="res%d" % h)
            nc.vector.tensor_tensor(res[:], logs[h][:, 1, :], logs[h][:, 0, :], ALU.subtract)
            nc.sync.dma_start(out=out[h * P : (h + 1) * P, :], in_=res[:])
